import numpy as np
import ml_dtypes


def mxq(x, axis, fmt="e4m3"):
    dtype, down = {"e4m3": (ml_dtypes.float8_e4m3fn, 7), "e5m2": (ml_dtypes.float8_e5m2, 14)}[fmt]
    v = np.moveaxis(np.asarray(x, np.float32).astype(ml_dtypes.bfloat16).astype(np.float64), axis, -1)
    blocks = v.reshape(v.shape[:-1] + (-1, 32))
    amax = np.abs(blocks).max(-1, keepdims=True)
    byte = np.maximum(np.where(amax > 0, np.frexp(amax)[1] - 1 + 127, 0) - down, 1)
    scale = np.exp2(byte - 127.0)
    codes = (blocks / scale).astype(np.float32).astype(dtype).astype(np.float64)
    return np.moveaxis((codes * scale).reshape(v.shape), -1, axis)


WIDE = False


def mx_kscale(k):
    if not WIDE:
        return np.ones(k)
    levels = np.array([10, -10, 5, -5, 0])
    if k % 512:
        return np.exp2(np.random.permutation(np.resize(levels, k // 32))).repeat(32)
    a = np.empty((k // 512, 16))
    for p in range(k // 512):
        a[p, :8] = np.random.permutation(np.resize(levels, 8))
        for g in range(8):
            far = levels[np.abs(levels - a[p, g]) >= 10]
            a[p, g + 8] = far[np.random.randint(len(far))]
    return np.exp2(a.ravel()).repeat(32)


def f64(x):
    return np.asarray(x).astype(np.float64)


def striped(idx):
    return np.tile(np.asarray(idx).reshape(-1, 16).T, (8, 1)).astype(np.uint16)


def unstriped(offs):
    return offs[:16].T.reshape(-1).astype(np.int64)


B, N, T, D, DV, NQ = 1, 512, 2048, 512, 256, 256
PAGE = 32
CAP = 2.0


def setup_inputs():
    n = np.random.standard_normal
    blocks = np.sort(np.stack([np.random.permutation(T // PAGE)[b::B][:N // PAGE] for b in range(B)]) * 0 + np.random.permutation(T // PAGE)[:B * N // PAGE].reshape(B, -1), axis=1)
    idx = (blocks[:, :, None] * PAGE + np.arange(PAGE)).reshape(-1)
    s = mx_kscale(D)[:, None]
    u = np.ones(T)
    u[idx] = mx_kscale(B * N)
    r = np.random.uniform(0.5, 2.0, T)
    k = n((D, T)) / s
    v = n((DV, T)) / (u * r)
    return {
        "qT": (n((B, D, NQ)) * s * (0.60 / np.sqrt(D))).astype(np.float32),
        "kT": k.astype(np.float32),
        "vT": v.astype(np.float32),
        "vs": np.tile(u * r, (128, 1)).astype(np.float32),
        "offs": striped(idx),
    }


def reference(qT, kT, vT, vs, offs):
    idx = unstriped(offs)
    k = f64(kT)
    v = f64(vT)
    pick = lambda x: x[:, idx].reshape(x.shape[0], B, N).transpose(1, 0, 2)
    q = f64(qT)
    score = mxq(q, 1, "e4m3").transpose(0, 2, 1) @ mxq(pick(k), 1, "e4m3")
    score = CAP * np.tanh(score / CAP)
    m = score.max(-1, keepdims=True)
    p = np.exp(score - m)
    total = p.sum(-1, keepdims=True)
    w = p * pick(f64(vs))[:, :1, :]
    y = mxq(w, 2, "e4m3") @ mxq(pick(v).transpose(0, 2, 1), 1, "e4m3")
    y = y / total
    return y

@@ -1,0 +1,213 @@
+from contextlib import ExitStack
+
+import concourse.mybir as mybir
+from concourse.masks import make_identity
+
+P = 128
+PACK = 4
+T = 2048
+N = 512
+D = 512
+DV = 256
+NQ = 256
+HALF = N // 2
+
+FLOPS = 2 * NQ * N * D + 2 * NQ * N * DV
+BYTES = 4 * (D * NQ + D * T + DV * T + T + NQ * DV) + 2 * P * (N // 16)
+
+F32 = mybir.dt.float32
+BF16 = mybir.dt.bfloat16
+U32 = mybir.dt.uint32
+U16 = mybir.dt.uint16
+U8 = mybir.dt.uint8
+FP8X4 = mybir.dt.float8_e4m3fn_x4
+
+ACT = mybir.ActivationFunctionType
+ALU = mybir.AluOpType
+AX = mybir.AxisListType
+
+
+def tile_attend_nsa_blk32_cap_kernel(tc, qT, kT, vT, vs, offs, out):
+    nc = tc.nc
+    out2 = out.rearrange("b q e -> (b q) e")
+    k_rows = kT.rearrange("(p t) n -> p t n", t=PACK)
+
+    with ExitStack() as ctx:
+        keep = ctx.enter_context(tc.tile_pool(name="keep", bufs=1))
+        psum = ctx.enter_context(tc.psum_pool(name="psum", bufs=8))
+
+        offsets = keep.tile([P, N // 16], U16, name="offsets")
+        nc.sync.dma_start(offsets[:], offs)
+
+        vs_win = keep.tile([P, T], F32, name="vs_win")
+        nc.gpsimd.memset(vs_win[:], 0.0)
+        ident = keep.tile([P, P], F32, name="ident")
+        make_identity(nc, ident[:])
+
+        warm = keep.tile([P, 1], F32, name="warm")
+        nc.vector.memset(warm[:], 0.0)
+        warm2 = keep.tile([P, 1], F32, name="warm2")
+        nc.scalar.activation(warm2[:], warm[:], ACT.Exp)
+
+        q_raw = keep.tile([P, PACK, NQ], F32, name="q_raw")
+        nc.sync.dma_start(q_raw[:], qT.rearrange("b (p j) q -> p (b j) q", j=PACK))
+
+        k_win = []
+        for t in range(PACK):
+            kw = keep.tile([P, T], F32, name=f"k_win{t}")
+            nc.sync.dma_start(kw[:], k_rows[:, t, :])
+            k_win.append(kw)
+            if t == 1:
+                nc.sync.dma_start(vs_win[0:1, :], vs[0:1, :])
+        v_win = []
+        for h in range(2):
+            vw = keep.tile([P, T], F32, name=f"v_win{h}")
+            nc.sync.dma_start(vw[:], vT[h * P : (h + 1) * P, :])
+            v_win.append(vw)
+
+        q_grp = keep.tile([P, NQ, PACK], BF16, name="q_grp", align_bytes=64)
+        nc.scalar.copy(q_grp[:], q_raw[:].rearrange("p j q -> p q j"))
+        q_codes = keep.tile([P, NQ], U32, name="q_codes", align_bytes=64)
+        q_scales = keep.tile([P, NQ], U8, name="q_scales", align_bytes=64)
+        nc.vector.quantize_mx(
+            out=q_codes[:].bitcast(FP8X4), scales=q_scales[:], in_=q_grp[:].rearrange("p q j -> p (q j)")
+        )
+
+        k_grp = keep.tile([P, N, PACK], BF16, name="k_grp", align_bytes=64)
+        vs_got = keep.tile([P, N], F32, name="vs_got")
+        vs4 = keep.tile([P, 1, PACK], F32, name="vs4")
+        for t in range(PACK):
+            nc.vector.tensor_copy(k_grp[:, :, t], k_win[t][:].indirect(offsets[:]))
+            if t == 1:
+                nc.vector.tensor_copy(vs_got[:], vs_win[:].indirect(offsets[:]))
+                vs_ps = psum.tile([P, PACK, P], F32, name="vs_ps", tag="bank")
+                for u in range(PACK):
+                    nc.tensor.transpose(vs_ps[:, u, :], vs_got[:, u::PACK], ident[:])
+                nc.vector.tensor_copy(vs4[:].rearrange("p o t -> p t o"), vs_ps[:, :, 0:1])
+
+        k_codes = keep.tile([P, N], U32, name="k_codes", align_bytes=64)
+        k_scales = keep.tile([P, N], U8, name="k_scales", align_bytes=64)
+        scores = {}
+        for h in range(2):
+            cols = slice(h * HALF, (h + 1) * HALF)
+            nc.vector.quantize_mx(
+                out=k_codes[:, cols].bitcast(FP8X4),
+                scales=k_scales[:, cols],
+                in_=k_grp[:, cols, :].rearrange("p s t -> p (s t)"),
+            )
+            for m in range(2):
+                rows = slice(m * P, (m + 1) * P)
+                sc = psum.tile([P, HALF], F32, name=f"sc{m}{h}", tag="bank")
+                nc.tensor.matmul_mx(
+                    out=sc[:],
+                    lhsT=q_codes[:, rows].bitcast(FP8X4),
+                    lhsT_scale=q_scales[:, rows],
+                    rhs=k_codes[:, cols].bitcast(FP8X4),
+                    rhs_scale=k_scales[:, cols],
+                    start=True,
+                    stop=True,
+                )
+                scores[m, h] = sc
+
+        v_codes = keep.tile([P, DV], U32, name="v_codes", align_bytes=64)
+        v_scales = keep.tile([P, DV], U8, name="v_scales", align_bytes=64)
+
+        def values_gather(h):
+            vg = keep.tile([P, N], F32, name=f"v_got{h}")
+            nc.vector.tensor_copy(vg[:], v_win[h][:].indirect(offsets[:]))
+            v_ps = psum.tile([P, PACK, P], F32, name=f"v_ps{h}", tag="bank")
+            for t in range(PACK):
+                nc.tensor.transpose(v_ps[:, t, :], vg[:, t::PACK], ident[:])
+            return v_ps
+
+        def values_quantize(h, v_ps):
+            vgr = keep.tile([P, P, PACK], BF16, name=f"vgr{h}", align_bytes=64)
+            nc.scalar.copy(vgr[:], v_ps[:].rearrange("s t e -> s e t"))
+            cols = slice(h * P, (h + 1) * P)
+            nc.vector.quantize_mx(
+                out=v_codes[:, cols].bitcast(FP8X4), scales=v_scales[:, cols], in_=vgr[:].rearrange("s e t -> s (e t)")
+            )
+
+        vp0 = values_gather(0)
+
+        cap = []
+        top = []
+        for m in range(2):
+            th = keep.tile([P, PACK, P], F32, name=f"cap{m}")
+            for h in range(2):
+                nc.scalar.activation(
+                    th[:, :, h * 64 : (h + 1) * 64],
+                    scores[m, h][:].rearrange("q (s t) -> q t s", t=PACK),
+                    ACT.Tanh,
+                    scale=0.5,
+                )
+            mx = keep.tile([P, 1], F32, name=f"max{m}")
+            nc.vector.reduce_max(mx[:], th[:].rearrange("q t s -> q (t s)"), axis=AX.X)
+            ng = keep.tile([P, 1], F32, name=f"neg{m}")
+            nc.vector.tensor_scalar_mul(ng[:], mx[:], -2.0)
+            cap.append(th)
+            top.append(ng)
+
+        p_t = []
+        inv = []
+        for m in range(2):
+            pm = keep.tile([P, PACK, P], F32, name=f"p{m}")
+            tot = keep.tile([P, 1], F32, name=f"tot{m}")
+            nc.scalar.activation(
+                pm[:].rearrange("q t s -> q (t s)"),
+                cap[m][:].rearrange("q t s -> q (t s)"),
+                ACT.Exp,
+                bias=top[m][:],
+                scale=2.0,
+                accum_out=tot[:],
+            )
+            p_t.append(pm)
+            inv.append(tot)
+
+        w_codes = keep.tile([P, NQ], U32, name="w_codes", align_bytes=64)
+        w_scales = keep.tile([P, NQ], U8, name="w_scales", align_bytes=64)
+
+        def weights(m):
+            pT = psum.tile([P, PACK, P], F32, name=f"pT{m}", tag="bank")
+            for t in range(PACK):
+                nc.tensor.transpose(pT[:, t, :], p_t[m][:, t, :], ident[:])
+            wg = keep.tile([P, P, PACK], BF16, name=f"wg{m}", align_bytes=64)
+            nc.vector.tensor_tensor(
+                wg[:], pT[:].rearrange("s t q -> s q t"), vs4[:].to_broadcast([P, P, PACK]), ALU.mult
+            )
+            cols = slice(m * P, (m + 1) * P)
+            nc.vector.quantize_mx(
+                out=w_codes[:, cols].bitcast(FP8X4), scales=w_scales[:, cols], in_=wg[:].rearrange("s q t -> s (q t)")
+            )
+            rc = keep.tile([P, 1], F32, name=f"rc{m}")
+            nc.vector.reciprocal(rc[:], inv[m][:])
+            return rc
+
+        rc = []
+        vp1 = values_gather(1)
+        rc.append(weights(0))
+        values_quantize(0, vp0)
+        rc.append(weights(1))
+        values_quantize(1, vp1)
+
+        for h in range(2):
+            ecols = slice(h * P, (h + 1) * P)
+            for m in range(2):
+                rows = slice(m * P, (m + 1) * P)
+                y_ps = psum.tile([P, P], F32, name=f"y_ps{m}{h}", tag="bank")
+                nc.tensor.matmul_mx(
+                    out=y_ps[:],
+                    lhsT=w_codes[:, rows].bitcast(FP8X4),
+                    lhsT_scale=w_scales[:, rows],
+                    rhs=v_codes[:, ecols].bitcast(FP8X4),
+                    rhs_scale=v_scales[:, ecols],
+                    start=True,
+                    stop=True,
+                )
+                y = keep.tile([P, P], F32, name=f"y{m}{h}")
+                if m == 0:
+                    nc.vector.tensor_scalar_mul(y[:], y_ps[:], rc[m][:])
+                    nc.sync.dma_start(out2[rows, ecols], y[:])
+                else:
+                    nc.scalar.activation(y[:], y_ps[:], ACT.Copy, scale=rc[m][:])
+                    nc.scalar.dma_start(out2[rows, ecols], y[:])

@@ -24,7 +24,6 @@ FP8X4 = mybir.dt.float8_e4m3fn_x4
 
 ACT = mybir.ActivationFunctionType
 ALU = mybir.AluOpType
-AX = mybir.AxisListType
 
 
 def tile_attend_nsa_blk32_cap_kernel(tc, qT, kT, vT, vs, offs, out):
@@ -36,6 +35,12 @@ def tile_attend_nsa_blk32_cap_kernel(tc, qT, kT, vT, vs, offs, out):
         keep = ctx.enter_context(tc.tile_pool(name="keep", bufs=1))
         psum = ctx.enter_context(tc.psum_pool(name="psum", bufs=8))
 
+        def bank(name, dtype=F32):
+            return psum.tile([P, PACK, P], dtype, name=name, tag="bank")
+
+        def quantize(codes, scales, cols, grouped):
+            nc.vector.quantize_mx(out=codes[:, cols].bitcast(FP8X4), scales=scales[:, cols], in_=grouped)
+
         offsets = keep.tile([P, N // 16], U16, name="offsets")
         nc.sync.dma_start(offsets[:], offs)
 
@@ -43,35 +48,28 @@ def tile_attend_nsa_blk32_cap_kernel(tc, qT, kT, vT, vs, offs, out):
         nc.gpsimd.memset(vs_win[:], 0.0)
         ident = keep.tile([P, P], F32, name="ident")
         make_identity(nc, ident[:])
+        ident_b = keep.tile([P, P], BF16, name="ident_b")
+        nc.vector.tensor_copy(ident_b[:], ident[:])
 
         warm = keep.tile([P, 1], F32, name="warm")
         nc.vector.memset(warm[:], 0.0)
         warm2 = keep.tile([P, 1], F32, name="warm2")
         nc.scalar.activation(warm2[:], warm[:], ACT.Exp)
 
-        q_raw = keep.tile([P, PACK, NQ], F32, name="q_raw")
-        nc.sync.dma_start(q_raw[:], qT.rearrange("b (p j) q -> p (b j) q", j=PACK))
-
         k_win = []
         for t in range(PACK):
-            kw = keep.tile([P, T], F32, name=f"k_win{t}")
+            kw = keep.tile([P, T], F32, name=f"k_win{t}", tag=f"k_win{t}", align_bytes=64)
             nc.sync.dma_start(kw[:], k_rows[:, t, :])
             k_win.append(kw)
             if t == 1:
                 nc.sync.dma_start(vs_win[0:1, :], vs[0:1, :])
+        q_raw = keep.tile([P, PACK, NQ], F32, name="q_raw")
+        nc.sync.dma_start(q_raw[:], qT.rearrange("b (p j) q -> p (b j) q", j=PACK))
         v_win = []
         for h in range(2):
             vw = keep.tile([P, T], F32, name=f"v_win{h}")
             nc.sync.dma_start(vw[:], vT[h * P : (h + 1) * P, :])
             v_win.append(vw)
-
-        q_grp = keep.tile([P, NQ, PACK], BF16, name="q_grp", align_bytes=64)
-        nc.scalar.copy(q_grp[:], q_raw[:].rearrange("p j q -> p q j"))
-        q_codes = keep.tile([P, NQ], U32, name="q_codes", align_bytes=64)
-        q_scales = keep.tile([P, NQ], U8, name="q_scales", align_bytes=64)
-        nc.vector.quantize_mx(
-            out=q_codes[:].bitcast(FP8X4), scales=q_scales[:], in_=q_grp[:].rearrange("p q j -> p (q j)")
-        )
 
         k_grp = keep.tile([P, N, PACK], BF16, name="k_grp", align_bytes=64)
         vs_got = keep.tile([P, N], F32, name="vs_got")
@@ -80,23 +78,32 @@ def tile_attend_nsa_blk32_cap_kernel(tc, qT, kT, vT, vs, offs, out):
             nc.vector.tensor_copy(k_grp[:, :, t], k_win[t][:].indirect(offsets[:]))
             if t == 1:
                 nc.vector.tensor_copy(vs_got[:], vs_win[:].indirect(offsets[:]))
-                vs_ps = psum.tile([P, PACK, P], F32, name="vs_ps", tag="bank")
+                vs_ps = bank("vs_ps")
                 for u in range(PACK):
                     nc.tensor.transpose(vs_ps[:, u, :], vs_got[:, u::PACK], ident[:])
+            if t == 2:
                 nc.vector.tensor_copy(vs4[:].rearrange("p o t -> p t o"), vs_ps[:, :, 0:1])
 
         k_codes = keep.tile([P, N], U32, name="k_codes", align_bytes=64)
         k_scales = keep.tile([P, N], U8, name="k_scales", align_bytes=64)
-        scores = {}
         for h in range(2):
             cols = slice(h * HALF, (h + 1) * HALF)
-            nc.vector.quantize_mx(
-                out=k_codes[:, cols].bitcast(FP8X4),
-                scales=k_scales[:, cols],
-                in_=k_grp[:, cols, :].rearrange("p s t -> p (s t)"),
-            )
-            for m in range(2):
-                rows = slice(m * P, (m + 1) * P)
+            quantize(k_codes, k_scales, cols, k_grp[:, cols, :].rearrange("p s t -> p (s t)"))
+
+        q_codes = keep.tile([P, NQ], U32, name="q_codes", tag="k_win3", align_bytes=64)
+        q_scales = keep.tile([P, NQ], U8, name="q_scales", align_bytes=64)
+        q_grp = []
+        for m in range(2):
+            rows = slice(m * P, (m + 1) * P)
+            qg = keep.tile([P, P, PACK], BF16, name=f"q_grp{m}", tag=f"q_grp{m}", align_bytes=64)
+            nc.scalar.copy(qg[:], q_raw[:, :, rows].rearrange("p j q -> p q j"))
+            quantize(q_codes, q_scales, rows, qg[:].rearrange("p q j -> p (q j)"))
+
+        scores = {}
+        for m in range(2):
+            rows = slice(m * P, (m + 1) * P)
+            for h in range(2):
+                cols = slice(h * HALF, (h + 1) * HALF)
                 sc = psum.tile([P, HALF], F32, name=f"sc{m}{h}", tag="bank")
                 nc.tensor.matmul_mx(
                     out=sc[:],
@@ -112,28 +119,29 @@ def tile_attend_nsa_blk32_cap_kernel(tc, qT, kT, vT, vs, offs, out):
         v_codes = keep.tile([P, DV], U32, name="v_codes", align_bytes=64)
         v_scales = keep.tile([P, DV], U8, name="v_scales", align_bytes=64)
 
-        def values_gather(h):
-            vg = keep.tile([P, N], F32, name=f"v_got{h}")
-            nc.vector.tensor_copy(vg[:], v_win[h][:].indirect(offsets[:]))
-            v_ps = psum.tile([P, PACK, P], F32, name=f"v_ps{h}", tag="bank")
+        def values_gather(h, tag):
+            vg = keep.tile([P, PACK, P], BF16, name=f"v_got{h}", tag=tag, align_bytes=64)
+            nc.vector.tensor_copy(vg[:].rearrange("e t s -> e s t"), v_win[h][:].indirect(offsets[:]))
+            return vg
+
+        def values_turn(h, vg):
+            v_ps = bank(f"v_ps{h}", BF16)
             for t in range(PACK):
-                nc.tensor.transpose(v_ps[:, t, :], vg[:, t::PACK], ident[:])
+                nc.tensor.transpose(v_ps[:, t, :], vg[:, t, :], ident_b[:])
             return v_ps
 
-        def values_quantize(h, v_ps):
-            vgr = keep.tile([P, P, PACK], BF16, name=f"vgr{h}", align_bytes=64)
+        def values_quantize(h, v_ps, tag):
+            vgr = keep.tile([P, P, PACK], BF16, name=f"vgr{h}", tag=tag, align_bytes=64)
             nc.scalar.copy(vgr[:], v_ps[:].rearrange("s t e -> s e t"))
-            cols = slice(h * P, (h + 1) * P)
-            nc.vector.quantize_mx(
-                out=v_codes[:, cols].bitcast(FP8X4), scales=v_scales[:, cols], in_=vgr[:].rearrange("s e t -> s (e t)")
-            )
+            quantize(v_codes, v_scales, slice(h * P, (h + 1) * P), vgr[:].rearrange("s e t -> s (e t)"))
 
-        vp0 = values_gather(0)
+        vg0 = values_gather(0, "q_grp1")
+        vp0 = values_turn(0, vg0)
 
         cap = []
         top = []
         for m in range(2):
-            th = keep.tile([P, PACK, P], F32, name=f"cap{m}")
+            th = keep.tile([P, PACK, P], F32, name=f"cap{m}", tag=f"cap{m}", align_bytes=64)
             for h in range(2):
                 nc.scalar.activation(
                     th[:, :, h * 64 : (h + 1) * 64],
@@ -141,12 +149,14 @@ def tile_attend_nsa_blk32_cap_kernel(tc, qT, kT, vT, vs, offs, out):
                     ACT.Tanh,
                     scale=0.5,
                 )
-            mx = keep.tile([P, 1], F32, name=f"max{m}")
-            nc.vector.reduce_max(mx[:], th[:].rearrange("q t s -> q (t s)"), axis=AX.X)
+            scrap = keep.tile([P, PACK * P], F32, name=f"scrap{m}", tag=f"scrap{m}", align_bytes=64)
             ng = keep.tile([P, 1], F32, name=f"neg{m}")
-            nc.vector.tensor_scalar_mul(ng[:], mx[:], -2.0)
+            nc.vector.tensor_scalar(
+                scrap[:], th[:].rearrange("q t s -> q (t s)"), -2.0, None, ALU.mult, ALU.min, accum_out=ng[:]
+            )
             cap.append(th)
             top.append(ng)
+        vg1 = values_gather(1, "scrap1")
 
         p_t = []
         inv = []
@@ -167,28 +177,23 @@ def tile_attend_nsa_blk32_cap_kernel(tc, qT, kT, vT, vs, offs, out):
         w_codes = keep.tile([P, NQ], U32, name="w_codes", align_bytes=64)
         w_scales = keep.tile([P, NQ], U8, name="w_scales", align_bytes=64)
 
-        def weights(m):
-            pT = psum.tile([P, PACK, P], F32, name=f"pT{m}", tag="bank")
+        rc = []
+        for m in range(2):
+            pT = bank(f"pT{m}")
             for t in range(PACK):
                 nc.tensor.transpose(pT[:, t, :], p_t[m][:, t, :], ident[:])
             wg = keep.tile([P, P, PACK], BF16, name=f"wg{m}", align_bytes=64)
             nc.vector.tensor_tensor(
                 wg[:], pT[:].rearrange("s t q -> s q t"), vs4[:].to_broadcast([P, P, PACK]), ALU.mult
             )
-            cols = slice(m * P, (m + 1) * P)
-            nc.vector.quantize_mx(
-                out=w_codes[:, cols].bitcast(FP8X4), scales=w_scales[:, cols], in_=wg[:].rearrange("s q t -> s (q t)")
-            )
-            rc = keep.tile([P, 1], F32, name=f"rc{m}")
-            nc.vector.reciprocal(rc[:], inv[m][:])
-            return rc
-
-        rc = []
-        vp1 = values_gather(1)
-        rc.append(weights(0))
-        values_quantize(0, vp0)
-        rc.append(weights(1))
-        values_quantize(1, vp1)
+            r = keep.tile([P, 1], F32, name=f"rc{m}")
+            nc.vector.reciprocal(r[:], inv[m][:])
+            rc.append(r)
+            quantize(w_codes, w_scales, slice(m * P, (m + 1) * P), wg[:].rearrange("s q t -> s (q t)"))
+            if m == 0:
+                values_quantize(0, vp0, "cap1")
+        vp1 = values_turn(1, vg1)
+        values_quantize(1, vp1, "vgr1")
 
         for h in range(2):
             ecols = slice(h * P, (h + 1) * P)

@@ -67,7 +67,7 @@ def tile_attend_nsa_blk32_cap_kernel(tc, qT, kT, vT, vs, offs, out):
         nc.sync.dma_start(q_raw[:], qT.rearrange("b (p j) q -> p (b j) q", j=PACK))
         v_win = []
         for h in range(2):
-            vw = keep.tile([P, T], F32, name=f"v_win{h}")
+            vw = keep.tile([P, T], F32, name=f"v_win{h}", tag=f"v_win{h}", align_bytes=64)
             nc.sync.dma_start(vw[:], vT[h * P : (h + 1) * P, :])
             v_win.append(vw)
 
@@ -149,7 +149,7 @@ def tile_attend_nsa_blk32_cap_kernel(tc, qT, kT, vT, vs, offs, out):
                     ACT.Tanh,
                     scale=0.5,
                 )
-            scrap = keep.tile([P, PACK * P], F32, name=f"scrap{m}", tag=f"scrap{m}", align_bytes=64)
+            scrap = keep.tile([P, PACK * P], F32, name=f"scrap{m}", tag=("v_win0" if m == 0 else "scrap1"), align_bytes=64)
             ng = keep.tile([P, 1], F32, name=f"neg{m}")
             nc.vector.tensor_scalar(
                 scrap[:], th[:].rearrange("q t s -> q (t s)"), -2.0, None, ALU.mult, ALU.min, accum_out=ng[:]
@@ -159,39 +159,35 @@ def tile_attend_nsa_blk32_cap_kernel(tc, qT, kT, vT, vs, offs, out):
         vg1 = values_gather(1, "scrap1")
 
         p_t = []
-        inv = []
+        tot2 = keep.tile([P, 2], F32, name="tot2")
         for m in range(2):
             pm = keep.tile([P, PACK, P], F32, name=f"p{m}")
-            tot = keep.tile([P, 1], F32, name=f"tot{m}")
             nc.scalar.activation(
                 pm[:].rearrange("q t s -> q (t s)"),
                 cap[m][:].rearrange("q t s -> q (t s)"),
                 ACT.Exp,
                 bias=top[m][:],
                 scale=2.0,
-                accum_out=tot[:],
+                accum_out=tot2[:, m : m + 1],
             )
             p_t.append(pm)
-            inv.append(tot)
 
         w_codes = keep.tile([P, NQ], U32, name="w_codes", align_bytes=64)
         w_scales = keep.tile([P, NQ], U8, name="w_scales", align_bytes=64)
 
-        rc = []
         for m in range(2):
             pT = bank(f"pT{m}")
             for t in range(PACK):
                 nc.tensor.transpose(pT[:, t, :], p_t[m][:, t, :], ident[:])
-            wg = keep.tile([P, P, PACK], BF16, name=f"wg{m}", align_bytes=64)
+            wg = keep.tile([P, P, PACK], BF16, name=f"wg{m}", tag=("v_win1" if m == 0 else "wg1"), align_bytes=64)
             nc.vector.tensor_tensor(
                 wg[:], pT[:].rearrange("s t q -> s q t"), vs4[:].to_broadcast([P, P, PACK]), ALU.mult
             )
-            r = keep.tile([P, 1], F32, name=f"rc{m}")
-            nc.vector.reciprocal(r[:], inv[m][:])
-            rc.append(r)
             quantize(w_codes, w_scales, slice(m * P, (m + 1) * P), wg[:].rearrange("s q t -> s (q t)"))
             if m == 0:
                 values_quantize(0, vp0, "cap1")
+        rc2 = keep.tile([P, 2], F32, name="rc2")
+        nc.vector.reciprocal(rc2[:], tot2[:])
         vp1 = values_turn(1, vg1)
         values_quantize(1, vp1, "vgr1")
 
@@ -211,8 +207,8 @@ def tile_attend_nsa_blk32_cap_kernel(tc, qT, kT, vT, vs, offs, out):
                 )
                 y = keep.tile([P, P], F32, name=f"y{m}{h}")
                 if m == 0:
-                    nc.vector.tensor_scalar_mul(y[:], y_ps[:], rc[m][:])
+                    nc.vector.tensor_scalar_mul(y[:], y_ps[:], rc2[:, m : m + 1])
                     nc.sync.dma_start(out2[rows, ecols], y[:])
                 else:
-                    nc.scalar.activation(y[:], y_ps[:], ACT.Copy, scale=rc[m][:])
+                    nc.scalar.activation(y[:], y_ps[:], ACT.Copy, scale=rc2[:, m : m + 1])
                     nc.scalar.dma_start(out2[rows, ecols], y[:])

@@ -10,6 +10,7 @@ N = 512
 D = 512
 DV = 256
 NQ = 256
+TILES = 2
 HALF = N // 2
 
 FLOPS = 2 * NQ * N * D + 2 * NQ * N * DV
@@ -28,7 +29,7 @@ ALU = mybir.AluOpType
 
 def tile_attend_nsa_blk32_cap_kernel(tc, qT, kT, vT, vs, offs, out):
     nc = tc.nc
-    out2 = out.rearrange("b q e -> (b q) e")
+    out_rows = out.rearrange("b q e -> (b q) e")
     k_rows = kT.rearrange("(p t) n -> p t n", t=PACK)
 
     with ExitStack() as ctx:
@@ -41,6 +42,17 @@ def tile_attend_nsa_blk32_cap_kernel(tc, qT, kT, vT, vs, offs, out):
         def quantize(codes, scales, cols, grouped):
             nc.vector.quantize_mx(out=codes[:, cols].bitcast(FP8X4), scales=scales[:, cols], in_=grouped)
 
+        def multiply(result, left, left_cols, right, right_cols):
+            nc.tensor.matmul_mx(
+                out=result,
+                lhsT=left[0][:, left_cols].bitcast(FP8X4),
+                lhsT_scale=left[1][:, left_cols],
+                rhs=right[0][:, right_cols].bitcast(FP8X4),
+                rhs_scale=right[1][:, right_cols],
+                start=True,
+                stop=True,
+            )
+
         offsets = keep.tile([P, N // 16], U16, name="offsets")
         nc.sync.dma_start(offsets[:], offs)
 
@@ -51,29 +63,29 @@ def tile_attend_nsa_blk32_cap_kernel(tc, qT, kT, vT, vs, offs, out):
         ident_b = keep.tile([P, P], BF16, name="ident_b")
         nc.vector.tensor_copy(ident_b[:], ident[:])
 
-        warm = keep.tile([P, 1], F32, name="warm")
-        nc.vector.memset(warm[:], 0.0)
-        warm2 = keep.tile([P, 1], F32, name="warm2")
-        nc.scalar.activation(warm2[:], warm[:], ACT.Exp)
+        table_in = keep.tile([P, 1], F32, name="table_in")
+        nc.vector.memset(table_in[:], 0.0)
+        table_out = keep.tile([P, 1], F32, name="table_out")
+        nc.scalar.activation(table_out[:], table_in[:], ACT.Exp)
 
         k_win = []
         for t in range(PACK):
-            kw = keep.tile([P, T], F32, name=f"k_win{t}", tag=f"k_win{t}", align_bytes=64)
-            nc.sync.dma_start(kw[:], k_rows[:, t, :])
-            k_win.append(kw)
+            plane = keep.tile([P, T], F32, name=f"k_win{t}", tag=f"k_win{t}", align_bytes=64)
+            nc.sync.dma_start(plane[:], k_rows[:, t, :])
+            k_win.append(plane)
             if t == 1:
                 nc.sync.dma_start(vs_win[0:1, :], vs[0:1, :])
         q_raw = keep.tile([P, PACK, NQ], F32, name="q_raw")
-        nc.sync.dma_start(q_raw[:], qT.rearrange("b (p j) q -> p (b j) q", j=PACK))
+        nc.sync.dma_start(q_raw[:], qT.rearrange("b (p t) q -> p (b t) q", t=PACK))
         v_win = []
-        for h in range(2):
-            vw = keep.tile([P, T], F32, name=f"v_win{h}", tag=f"v_win{h}", align_bytes=64)
-            nc.sync.dma_start(vw[:], vT[h * P : (h + 1) * P, :])
-            v_win.append(vw)
+        for h in range(TILES):
+            pool_rows = keep.tile([P, T], F32, name=f"v_win{h}", tag=f"v_win{h}", align_bytes=64)
+            nc.sync.dma_start(pool_rows[:], vT[h * P : (h + 1) * P, :])
+            v_win.append(pool_rows)
 
         k_grp = keep.tile([P, N, PACK], BF16, name="k_grp", align_bytes=64)
         vs_got = keep.tile([P, N], F32, name="vs_got")
-        vs4 = keep.tile([P, 1, PACK], F32, name="vs4")
+        vs_cols = keep.tile([P, 1, PACK], F32, name="vs_cols")
         for t in range(PACK):
             nc.vector.tensor_copy(k_grp[:, :, t], k_win[t][:].indirect(offsets[:]))
             if t == 1:
@@ -82,133 +94,124 @@ def tile_attend_nsa_blk32_cap_kernel(tc, qT, kT, vT, vs, offs, out):
                 for u in range(PACK):
                     nc.tensor.transpose(vs_ps[:, u, :], vs_got[:, u::PACK], ident[:])
             if t == 2:
-                nc.vector.tensor_copy(vs4[:].rearrange("p o t -> p t o"), vs_ps[:, :, 0:1])
+                nc.vector.tensor_copy(vs_cols[:].rearrange("p o t -> p t o"), vs_ps[:, :, 0:1])
 
         k_codes = keep.tile([P, N], U32, name="k_codes", align_bytes=64)
         k_scales = keep.tile([P, N], U8, name="k_scales", align_bytes=64)
-        for h in range(2):
-            cols = slice(h * HALF, (h + 1) * HALF)
-            quantize(k_codes, k_scales, cols, k_grp[:, cols, :].rearrange("p s t -> p (s t)"))
+        for part in range(N // HALF):
+            slots = slice(part * HALF, (part + 1) * HALF)
+            quantize(k_codes, k_scales, slots, k_grp[:, slots, :].rearrange("p i t -> p (i t)"))
 
         q_codes = keep.tile([P, NQ], U32, name="q_codes", tag="k_win3", align_bytes=64)
         q_scales = keep.tile([P, NQ], U8, name="q_scales", align_bytes=64)
-        q_grp = []
-        for m in range(2):
+        for m in range(TILES):
             rows = slice(m * P, (m + 1) * P)
-            qg = keep.tile([P, P, PACK], BF16, name=f"q_grp{m}", tag=f"q_grp{m}", align_bytes=64)
-            nc.scalar.copy(qg[:], q_raw[:, :, rows].rearrange("p j q -> p q j"))
-            quantize(q_codes, q_scales, rows, qg[:].rearrange("p q j -> p (q j)"))
+            q_grp = keep.tile([P, P, PACK], BF16, name=f"q_grp{m}", tag=f"q_grp{m}", align_bytes=64)
+            nc.scalar.copy(q_grp[:], q_raw[:, :, rows].rearrange("p t q -> p q t"))
+            quantize(q_codes, q_scales, rows, q_grp[:].rearrange("p q t -> p (q t)"))
 
         scores = {}
-        for m in range(2):
-            rows = slice(m * P, (m + 1) * P)
-            for h in range(2):
-                cols = slice(h * HALF, (h + 1) * HALF)
-                sc = psum.tile([P, HALF], F32, name=f"sc{m}{h}", tag="bank")
-                nc.tensor.matmul_mx(
-                    out=sc[:],
-                    lhsT=q_codes[:, rows].bitcast(FP8X4),
-                    lhsT_scale=q_scales[:, rows],
-                    rhs=k_codes[:, cols].bitcast(FP8X4),
-                    rhs_scale=k_scales[:, cols],
-                    start=True,
-                    stop=True,
+        for m in range(TILES):
+            for part in range(N // HALF):
+                sc = psum.tile([P, HALF], F32, name=f"sc{m}{part}", tag="bank")
+                multiply(
+                    sc[:],
+                    (q_codes, q_scales),
+                    slice(m * P, (m + 1) * P),
+                    (k_codes, k_scales),
+                    slice(part * HALF, (part + 1) * HALF),
                 )
-                scores[m, h] = sc
+                scores[m, part] = sc
 
         v_codes = keep.tile([P, DV], U32, name="v_codes", align_bytes=64)
         v_scales = keep.tile([P, DV], U8, name="v_scales", align_bytes=64)
 
         def values_gather(h, tag):
-            vg = keep.tile([P, PACK, P], BF16, name=f"v_got{h}", tag=tag, align_bytes=64)
-            nc.vector.tensor_copy(vg[:].rearrange("e t s -> e s t"), v_win[h][:].indirect(offsets[:]))
-            return vg
+            got = keep.tile([P, PACK, P], BF16, name=f"v_got{h}", tag=tag, align_bytes=64)
+            nc.vector.tensor_copy(got[:].rearrange("e t s -> e s t"), v_win[h][:].indirect(offsets[:]))
+            return got
 
-        def values_turn(h, vg):
+        def values_turn(h, got):
             v_ps = bank(f"v_ps{h}", BF16)
             for t in range(PACK):
-                nc.tensor.transpose(v_ps[:, t, :], vg[:, t, :], ident_b[:])
+                nc.tensor.transpose(v_ps[:, t, :], got[:, t, :], ident_b[:])
             return v_ps
 
-        def values_quantize(h, v_ps, tag):
-            vgr = keep.tile([P, P, PACK], BF16, name=f"vgr{h}", tag=tag, align_bytes=64)
-            nc.scalar.copy(vgr[:], v_ps[:].rearrange("s t e -> s e t"))
-            quantize(v_codes, v_scales, slice(h * P, (h + 1) * P), vgr[:].rearrange("s e t -> s (e t)"))
+        def values_quantize(h, v_ps, grouped):
+            nc.scalar.copy(grouped, v_ps[:].rearrange("s t e -> s e t"))
+            quantize(v_codes, v_scales, slice(h * P, (h + 1) * P), grouped.rearrange("s e t -> s (e t)"))
 
-        vg0 = values_gather(0, "q_grp1")
-        vp0 = values_turn(0, vg0)
+        v_turned0 = values_turn(0, values_gather(0, "q_grp1"))
 
-        cap = []
-        top = []
-        for m in range(2):
+        capped = []
+        neg_max = []
+        for m in range(TILES):
             th = keep.tile([P, PACK, P], F32, name=f"cap{m}", tag=f"cap{m}", align_bytes=64)
-            for h in range(2):
+            for part in range(N // HALF):
                 nc.scalar.activation(
-                    th[:, :, h * 64 : (h + 1) * 64],
-                    scores[m, h][:].rearrange("q (s t) -> q t s", t=PACK),
+                    th[:, :, part * (HALF // PACK) : (part + 1) * (HALF // PACK)],
+                    scores[m, part][:].rearrange("q (s t) -> q t s", t=PACK),
                     ACT.Tanh,
                     scale=0.5,
                 )
-            scrap = keep.tile([P, PACK * P], F32, name=f"scrap{m}", tag=("v_win0" if m == 0 else "scrap1"), align_bytes=64)
-            ng = keep.tile([P, 1], F32, name=f"neg{m}")
+            scrap_tag = "v_win0" if m == 0 else "scrap1"
+            scrap = keep.tile([P, PACK * P], F32, name=f"scrap{m}", tag=scrap_tag, align_bytes=64)
+            least = keep.tile([P, 1], F32, name=f"least{m}")
             nc.vector.tensor_scalar(
-                scrap[:], th[:].rearrange("q t s -> q (t s)"), -2.0, None, ALU.mult, ALU.min, accum_out=ng[:]
+                scrap[:], th[:].rearrange("q t s -> q (t s)"), -2.0, None, ALU.mult, ALU.min, accum_out=least[:]
             )
-            cap.append(th)
-            top.append(ng)
-        vg1 = values_gather(1, "scrap1")
+            capped.append(th)
+            neg_max.append(least)
+        v_got1 = values_gather(1, "scrap1")
 
-        p_t = []
-        tot2 = keep.tile([P, 2], F32, name="tot2")
-        for m in range(2):
-            pm = keep.tile([P, PACK, P], F32, name=f"p{m}")
+        p_rows = []
+        row_sums = keep.tile([P, TILES], F32, name="row_sums")
+        for m in range(TILES):
+            p_tile = keep.tile([P, PACK, P], F32, name=f"p{m}")
             nc.scalar.activation(
-                pm[:].rearrange("q t s -> q (t s)"),
-                cap[m][:].rearrange("q t s -> q (t s)"),
+                p_tile[:].rearrange("q t s -> q (t s)"),
+                capped[m][:].rearrange("q t s -> q (t s)"),
                 ACT.Exp,
-                bias=top[m][:],
+                bias=neg_max[m][:],
                 scale=2.0,
-                accum_out=tot2[:, m : m + 1],
+                accum_out=row_sums[:, m : m + 1],
             )
-            p_t.append(pm)
+            p_rows.append(p_tile)
 
+        late = keep.tile([P, 2, P, PACK], BF16, name="late", tag="v_win1", align_bytes=64)
         w_codes = keep.tile([P, NQ], U32, name="w_codes", align_bytes=64)
         w_scales = keep.tile([P, NQ], U8, name="w_scales", align_bytes=64)
-
-        for m in range(2):
-            pT = bank(f"pT{m}")
+        for m in range(TILES):
+            p_ps = bank(f"p_ps{m}")
             for t in range(PACK):
-                nc.tensor.transpose(pT[:, t, :], p_t[m][:, t, :], ident[:])
-            wg = keep.tile([P, P, PACK], BF16, name=f"wg{m}", tag=("v_win1" if m == 0 else "wg1"), align_bytes=64)
-            nc.vector.tensor_tensor(
-                wg[:], pT[:].rearrange("s t q -> s q t"), vs4[:].to_broadcast([P, P, PACK]), ALU.mult
-            )
-            quantize(w_codes, w_scales, slice(m * P, (m + 1) * P), wg[:].rearrange("s q t -> s (q t)"))
+                nc.tensor.transpose(p_ps[:, t, :], p_rows[m][:, t, :], ident[:])
             if m == 0:
-                values_quantize(0, vp0, "cap1")
-        rc2 = keep.tile([P, 2], F32, name="rc2")
-        nc.vector.reciprocal(rc2[:], tot2[:])
-        vp1 = values_turn(1, vg1)
-        values_quantize(1, vp1, "vgr1")
+                w_grp = late[:, 0]
+            else:
+                w_grp1 = keep.tile([P, P, PACK], BF16, name="w_grp1", align_bytes=64)
+                w_grp = w_grp1[:]
+            nc.vector.tensor_tensor(
+                w_grp, p_ps[:].rearrange("s t q -> s q t"), vs_cols[:].to_broadcast([P, P, PACK]), ALU.mult
+            )
+            quantize(w_codes, w_scales, slice(m * P, (m + 1) * P), w_grp.rearrange("s q t -> s (q t)"))
+            if m == 0:
+                values_quantize(0, v_turned0, late[:, 1])
+        v_turned1 = values_turn(1, v_got1)
+        inverse = keep.tile([P, TILES], F32, name="inverse", tag="scrap1", align_bytes=64)
+        nc.vector.reciprocal(inverse[:], row_sums[:])
+        v_grp1 = keep.tile([P, P, PACK], BF16, name="v_grp1", align_bytes=64)
+        values_quantize(1, v_turned1, v_grp1[:])
 
-        for h in range(2):
-            ecols = slice(h * P, (h + 1) * P)
-            for m in range(2):
+        for h in range(TILES):
+            features = slice(h * P, (h + 1) * P)
+            for m in range(TILES):
                 rows = slice(m * P, (m + 1) * P)
                 y_ps = psum.tile([P, P], F32, name=f"y_ps{m}{h}", tag="bank")
-                nc.tensor.matmul_mx(
-                    out=y_ps[:],
-                    lhsT=w_codes[:, rows].bitcast(FP8X4),
-                    lhsT_scale=w_scales[:, rows],
-                    rhs=v_codes[:, ecols].bitcast(FP8X4),
-                    rhs_scale=v_scales[:, ecols],
-                    start=True,
-                    stop=True,
-                )
+                multiply(y_ps[:], (w_codes, w_scales), rows, (v_codes, v_scales), features)
                 y = keep.tile([P, P], F32, name=f"y{m}{h}")
                 if m == 0:
-                    nc.vector.tensor_scalar_mul(y[:], y_ps[:], rc2[:, m : m + 1])
-                    nc.sync.dma_start(out2[rows, ecols], y[:])
+                    nc.vector.tensor_scalar_mul(y[:], y_ps[:], inverse[:, m : m + 1])
+                    nc.sync.dma_start(out_rows[rows, features], y[:])
                 else:
-                    nc.scalar.activation(y[:], y_ps[:], ACT.Copy, scale=rc2[:, m : m + 1])
-                    nc.scalar.dma_start(out2[rows, ecols], y[:])
+                    nc.scalar.activation(y[:], y_ps[:], ACT.Copy, scale=inverse[:, m : m + 1])
+                    nc.scalar.dma_start(out_rows[rows, features], y[:])

from contextlib import ExitStack

import concourse.mybir as mybir
from concourse.masks import make_identity

P = 128
PACK = 4
T = 2048
N = 512
D = 512
DV = 256
NQ = 256
TILES = 2
HALF = N // 2

FLOPS = 2 * NQ * N * D + 2 * NQ * N * DV
BYTES = 4 * (D * NQ + D * T + DV * T + T + NQ * DV) + 2 * P * (N // 16)

F32 = mybir.dt.float32
BF16 = mybir.dt.bfloat16
U32 = mybir.dt.uint32
U16 = mybir.dt.uint16
U8 = mybir.dt.uint8
FP8X4 = mybir.dt.float8_e4m3fn_x4

ACT = mybir.ActivationFunctionType
ALU = mybir.AluOpType


def tile_attend_nsa_blk32_cap_kernel(tc, qT, kT, vT, vs, offs, out):
    nc = tc.nc
    out_rows = out.rearrange("b q e -> (b q) e")
    k_rows = kT.rearrange("(p t) n -> p t n", t=PACK)

    with ExitStack() as ctx:
        keep = ctx.enter_context(tc.tile_pool(name="keep", bufs=1))
        psum = ctx.enter_context(tc.psum_pool(name="psum", bufs=8))

        def bank(name, dtype=F32):
            return psum.tile([P, PACK, P], dtype, name=name, tag="bank")

        def quantize(codes, scales, cols, grouped):
            nc.vector.quantize_mx(out=codes[:, cols].bitcast(FP8X4), scales=scales[:, cols], in_=grouped)

        def multiply(result, left, left_cols, right, right_cols):
            nc.tensor.matmul_mx(
                out=result,
                lhsT=left[0][:, left_cols].bitcast(FP8X4),
                lhsT_scale=left[1][:, left_cols],
                rhs=right[0][:, right_cols].bitcast(FP8X4),
                rhs_scale=right[1][:, right_cols],
                start=True,
                stop=True,
            )

        offsets = keep.tile([P, N // 16], U16, name="offsets")
        nc.sync.dma_start(offsets[:], offs)

        vs_win = keep.tile([P, T], F32, name="vs_win")
        nc.gpsimd.memset(vs_win[:], 0.0)
        ident = keep.tile([P, P], F32, name="ident")
        make_identity(nc, ident[:])
        ident_b = keep.tile([P, P], BF16, name="ident_b")
        nc.vector.tensor_copy(ident_b[:], ident[:])

        table_in = keep.tile([P, 1], F32, name="table_in")
        nc.vector.memset(table_in[:], 0.0)
        table_out = keep.tile([P, 1], F32, name="table_out")
        nc.scalar.activation(table_out[:], table_in[:], ACT.Exp)

        k_win = []
        for t in range(PACK):
            plane = keep.tile([P, T], F32, name=f"k_win{t}", tag=f"k_win{t}", align_bytes=64)
            nc.sync.dma_start(plane[:], k_rows[:, t, :])
            k_win.append(plane)
            if t == 1:
                nc.sync.dma_start(vs_win[0:1, :], vs[0:1, :])
        q_raw = keep.tile([P, PACK, NQ], F32, name="q_raw")
        nc.sync.dma_start(q_raw[:], qT.rearrange("b (p t) q -> p (b t) q", t=PACK))
        v_win = []
        for h in range(TILES):
            pool_rows = keep.tile([P, T], F32, name=f"v_win{h}", tag=f"v_win{h}", align_bytes=64)
            nc.sync.dma_start(pool_rows[:], vT[h * P : (h + 1) * P, :])
            v_win.append(pool_rows)

        k_grp = keep.tile([P, N, PACK], BF16, name="k_grp", align_bytes=64)
        vs_got = keep.tile([P, N], F32, name="vs_got")
        vs_cols = keep.tile([P, 1, PACK], F32, name="vs_cols")
        for t in range(PACK):
            nc.vector.tensor_copy(k_grp[:, :, t], k_win[t][:].indirect(offsets[:]))
            if t == 1:
                nc.vector.tensor_copy(vs_got[:], vs_win[:].indirect(offsets[:]))
                vs_ps = bank("vs_ps")
                for u in range(PACK):
                    nc.tensor.transpose(vs_ps[:, u, :], vs_got[:, u::PACK], ident[:])
            if t == 2:
                nc.vector.tensor_copy(vs_cols[:].rearrange("p o t -> p t o"), vs_ps[:, :, 0:1])

        k_codes = keep.tile([P, N], U32, name="k_codes", align_bytes=64)
        k_scales = keep.tile([P, N], U8, name="k_scales", align_bytes=64)
        for part in range(N // HALF):
            slots = slice(part * HALF, (part + 1) * HALF)
            quantize(k_codes, k_scales, slots, k_grp[:, slots, :].rearrange("p i t -> p (i t)"))

        q_codes = keep.tile([P, NQ], U32, name="q_codes", tag="k_win3", align_bytes=64)
        q_scales = keep.tile([P, NQ], U8, name="q_scales", align_bytes=64)
        for m in range(TILES):
            rows = slice(m * P, (m + 1) * P)
            q_grp = keep.tile([P, P, PACK], BF16, name=f"q_grp{m}", tag=f"q_grp{m}", align_bytes=64)
            nc.scalar.copy(q_grp[:], q_raw[:, :, rows].rearrange("p t q -> p q t"))
            quantize(q_codes, q_scales, rows, q_grp[:].rearrange("p q t -> p (q t)"))

        scores = {}
        for m in range(TILES):
            for part in range(N // HALF):
                sc = psum.tile([P, HALF], F32, name=f"sc{m}{part}", tag="bank")
                multiply(
                    sc[:],
                    (q_codes, q_scales),
                    slice(m * P, (m + 1) * P),
                    (k_codes, k_scales),
                    slice(part * HALF, (part + 1) * HALF),
                )
                scores[m, part] = sc

        v_codes = keep.tile([P, DV], U32, name="v_codes", align_bytes=64)
        v_scales = keep.tile([P, DV], U8, name="v_scales", align_bytes=64)

        def values_gather(h, tag):
            got = keep.tile([P, PACK, P], BF16, name=f"v_got{h}", tag=tag, align_bytes=64)
            nc.vector.tensor_copy(got[:].rearrange("e t s -> e s t"), v_win[h][:].indirect(offsets[:]))
            return got

        def values_turn(h, got):
            v_ps = bank(f"v_ps{h}", BF16)
            for t in range(PACK):
                nc.tensor.transpose(v_ps[:, t, :], got[:, t, :], ident_b[:])
            return v_ps

        def values_quantize(h, v_ps, grouped):
            nc.scalar.copy(grouped, v_ps[:].rearrange("s t e -> s e t"))
            quantize(v_codes, v_scales, slice(h * P, (h + 1) * P), grouped.rearrange("s e t -> s (e t)"))

        v_turned0 = values_turn(0, values_gather(0, "q_grp1"))

        capped = []
        neg_max = []
        for m in range(TILES):
            th = keep.tile([P, PACK, P], F32, name=f"cap{m}", tag=f"cap{m}", align_bytes=64)
            for part in range(N // HALF):
                nc.scalar.activation(
                    th[:, :, part * (HALF // PACK) : (part + 1) * (HALF // PACK)],
                    scores[m, part][:].rearrange("q (s t) -> q t s", t=PACK),
                    ACT.Tanh,
                    scale=0.5,
                )
            scrap_tag = "v_win0" if m == 0 else "scrap1"
            scrap = keep.tile([P, PACK * P], F32, name=f"scrap{m}", tag=scrap_tag, align_bytes=64)
            least = keep.tile([P, 1], F32, name=f"least{m}")
            nc.vector.tensor_scalar(
                scrap[:], th[:].rearrange("q t s -> q (t s)"), -2.0, None, ALU.mult, ALU.min, accum_out=least[:]
            )
            capped.append(th)
            neg_max.append(least)
        v_got1 = values_gather(1, "scrap1")

        p_rows = []
        row_sums = keep.tile([P, TILES], F32, name="row_sums")
        for m in range(TILES):
            p_tile = keep.tile([P, PACK, P], F32, name=f"p{m}")
            nc.scalar.activation(
                p_tile[:].rearrange("q t s -> q (t s)"),
                capped[m][:].rearrange("q t s -> q (t s)"),
                ACT.Exp,
                bias=neg_max[m][:],
                scale=2.0,
                accum_out=row_sums[:, m : m + 1],
            )
            p_rows.append(p_tile)

        late = keep.tile([P, 2, P, PACK], BF16, name="late", tag="v_win1", align_bytes=64)
        w_codes = keep.tile([P, NQ], U32, name="w_codes", align_bytes=64)
        w_scales = keep.tile([P, NQ], U8, name="w_scales", align_bytes=64)
        for m in range(TILES):
            p_ps = bank(f"p_ps{m}")
            for t in range(PACK):
                nc.tensor.transpose(p_ps[:, t, :], p_rows[m][:, t, :], ident[:])
            if m == 0:
                w_grp = late[:, 0]
            else:
                w_grp1 = keep.tile([P, P, PACK], BF16, name="w_grp1", align_bytes=64)
                w_grp = w_grp1[:]
            nc.vector.tensor_tensor(
                w_grp, p_ps[:].rearrange("s t q -> s q t"), vs_cols[:].to_broadcast([P, P, PACK]), ALU.mult
            )
            quantize(w_codes, w_scales, slice(m * P, (m + 1) * P), w_grp.rearrange("s q t -> s (q t)"))
            if m == 0:
                values_quantize(0, v_turned0, late[:, 1])
        v_turned1 = values_turn(1, v_got1)
        inverse = keep.tile([P, TILES], F32, name="inverse", tag="scrap1", align_bytes=64)
        nc.vector.reciprocal(inverse[:], row_sums[:])
        v_grp1 = keep.tile([P, P, PACK], BF16, name="v_grp1", align_bytes=64)
        values_quantize(1, v_turned1, v_grp1[:])

        for h in range(TILES):
            features = slice(h * P, (h + 1) * P)
            for m in range(TILES):
                rows = slice(m * P, (m + 1) * P)
                y_ps = psum.tile([P, P], F32, name=f"y_ps{m}{h}", tag="bank")
                multiply(y_ps[:], (w_codes, w_scales), rows, (v_codes, v_scales), features)
                y = keep.tile([P, P], F32, name=f"y{m}{h}")
                if m == 0:
                    nc.vector.tensor_scalar_mul(y[:], y_ps[:], inverse[:, m : m + 1])
                    nc.sync.dma_start(out_rows[rows, features], y[:])
                else:
                    nc.scalar.activation(y[:], y_ps[:], ACT.Copy, scale=inverse[:, m : m + 1])
                    nc.scalar.dma_start(out_rows[rows, features], y[:])
